import numpy as np
import ml_dtypes


def mxq(x, axis, fmt="e4m3"):
    dtype, down = {"e4m3": (ml_dtypes.float8_e4m3fn, 7), "e5m2": (ml_dtypes.float8_e5m2, 14)}[fmt]
    v = np.moveaxis(np.asarray(x, np.float32).astype(ml_dtypes.bfloat16).astype(np.float64), axis, -1)
    blocks = v.reshape(v.shape[:-1] + (-1, 32))
    amax = np.abs(blocks).max(-1, keepdims=True)
    byte = np.maximum(np.where(amax > 0, np.frexp(amax)[1] - 1 + 127, 0) - down, 1)
    scale = np.exp2(byte - 127.0)
    codes = (blocks / scale).astype(np.float32).astype(dtype).astype(np.float64)
    return np.moveaxis((codes * scale).reshape(v.shape), -1, axis)


WIDE = False


def mx_kscale(k):
    if not WIDE:
        return np.ones(k)
    levels = np.array([10, -10, 5, -5, 0])
    if k % 512:
        return np.exp2(np.random.permutation(np.resize(levels, k // 32))).repeat(32)
    a = np.empty((k // 512, 16))
    for p in range(k // 512):
        a[p, :8] = np.random.permutation(np.resize(levels, 8))
        for g in range(8):
            far = levels[np.abs(levels - a[p, g]) >= 10]
            a[p, g + 8] = far[np.random.randint(len(far))]
    return np.exp2(a.ravel()).repeat(32)


def f64(x):
    return np.asarray(x).astype(np.float64)


def striped(idx):
    return np.tile(idx.reshape(-1, 16).T, (8, 1)).astype(np.uint16)


def unstriped(offs):
    return offs[:16].T.reshape(-1).astype(np.int64)


def pack_weight(w):
    k, n = w.shape
    w = f64(np.asarray(w, np.float32).astype(ml_dtypes.bfloat16)).reshape(k // 32, 32, n)
    amax = np.abs(w).max(1)
    byte = np.clip(np.where(amax > 0, np.frexp(amax)[1] - 1 + 127 - 7, 1), 1, 254)
    scaled = (w * np.exp2(127.0 - byte)[:, None, :]).reshape(k, n).astype(np.float32)
    words = np.ascontiguousarray(scaled.reshape(k // 512, 128, 4, n).transpose(0, 1, 3, 2)).astype(ml_dtypes.float8_e4m3fn).view(np.uint8)
    return words, np.ascontiguousarray(byte.astype(np.uint8).reshape(k // 512, 16, n))


def unpack_weight(words, scales):
    g, p, n, _ = words.shape
    vals = np.ascontiguousarray(words).view(ml_dtypes.float8_e4m3fn).astype(np.float64) * np.repeat(np.exp2(scales.astype(np.float64) - 127.0), 8, axis=1)[..., None]
    return vals.transpose(0, 1, 3, 2).reshape(g * 512, n)


K, T, S, N, H, W = 512, 2048, 512, 512, 512, 384


def setup_inputs():
    n = np.random.standard_normal
    s = mx_kscale(K)[:, None]
    u = mx_kscale(S)
    packed_xT = pack_weight(n((K, T)) * s)
    return {
        "x_words": packed_xT[0],
        "x_scales": packed_xT[1],
        "wa": (n((K, H)) / np.sqrt(K) / s).astype(np.float32),
        "gt": (np.random.uniform(0.5, 1.5, (S, 1)) * u[:, None]).astype(np.float32),
        "w1": (n((S, N)) / np.sqrt(S) / u[:, None]).astype(np.float32),
        "offs": striped(np.random.permutation(T)[:S]),
        "n1": striped(np.random.permutation(H)),
        "n2": striped(np.random.permutation(H)),
        "n3": striped(np.random.permutation(H)[:W]),
        "n4": striped(np.random.permutation(H)[:W]),
    }


def reference(x_words, x_scales, wa, gt, w1, offs, n1, n2, n3, n4):
    xq = unpack_weight(x_words, x_scales)[:, unstriped(offs)]
    y = xq.T @ mxq(f64(wa), 0, "e4m3")
    z = f64(gt) * (np.minimum(np.maximum(y, y[:, unstriped(n1)]), y[:, unstriped(n2)]))
    h = mxq(f64(w1), 0, "e4m3").T @ mxq(z, 0, "e4m3")
    old = h[:, unstriped(n3)]
    pa = h[:, unstriped(n4)]
    ra = old / (np.abs(pa) + 0.5)
    out = h.copy()
    out[:, unstriped(n3)] = ra
    return out

@@ -1,0 +1,251 @@
+from contextlib import ExitStack
+
+import concourse.mybir as mybir
+
+K, T, S, N, H, W = 512, 2048, 512, 512, 512, 384
+FLOPS = 2 * K * S * H + 2 * S * N * H
+
+F32 = mybir.dt.float32
+BF16 = mybir.dt.bfloat16
+I32 = mybir.dt.int32
+U32 = mybir.dt.uint32
+U16 = mybir.dt.uint16
+U8 = mybir.dt.uint8
+FP8X4 = mybir.dt.float8_e4m3fn_x4
+ALU = mybir.AluOpType
+ACT = mybir.ActivationFunctionType
+
+P = 128
+PACK = 4
+HALF = H // 2
+RUN = 4
+
+
+def packed_view(tile):
+    return tile.rearrange("p (c i) t -> p c t i", i=RUN)
+
+
+def planes_view(ap):
+    return ap.rearrange("p t (c i) -> p c t i", i=RUN)
+
+
+def tile_picked_tokminmxknorm_none_p_kernel(
+    tc, x_words, x_scales, wa, gt, w1, offs, n1, n2, n3, n4, out
+):
+    nc = tc.nc
+    with ExitStack() as ctx:
+        lists = ctx.enter_context(tc.tile_pool(name="lists", bufs=1))
+        keep = ctx.enter_context(tc.tile_pool(name="keep", bufs=1))
+        psum = ctx.enter_context(tc.psum_pool(name="psum", bufs=1))
+
+        def quantise(grouped, width, name):
+            codes = keep.tile([P, width], U32, align_bytes=64, name=name + "_codes")
+            scales = keep.tile([P, width], U8, align_bytes=64, name=name + "_scales")
+            nc.vector.quantize_mx(
+                out=codes[:].bitcast(FP8X4), scales=scales[:], in_=grouped[:].rearrange("p c t -> p (c t)")
+            )
+            return codes, scales
+
+        wa_rows = wa.rearrange("(p t) w -> p t w", t=PACK)
+        wa_raw = [keep.tile([P, PACK, HALF], F32, name="wa_raw%d" % f) for f in range(2)]
+        nc.sync.dma_start(out=wa_raw[0][:], in_=wa_rows[:, :, 0:HALF])
+        table_scales = keep.tile([P, T], U8, name="table_scales")
+        nc.gpsimd.memset(table_scales[:].bitcast(I32), 0)
+        for q in range(4):
+            nc.sync.dma_start(
+                out=table_scales[32 * q : 32 * q + 4, :].bitcast(I32),
+                in_=x_scales[0, 4 * q : 4 * q + 4, :].bitcast(I32),
+            )
+        offs_sb = lists.tile([P, S // 16], U16, name="offs_sb")
+        nc.sync.dma_start(offs_sb[:], offs)
+        table_words = keep.tile([P, T], U32, name="table_words")
+        nc.sync.dma_start(
+            out=table_words[:].bitcast(I32), in_=x_words[0].rearrange("p n t -> p (n t)").bitcast(I32)
+        )
+        nc.sync.dma_start(out=wa_raw[1][:], in_=wa_rows[:, :, HALF:H])
+        gate = keep.tile([P, PACK], F32, name="gate")
+        nc.sync.dma_start(out=gate[:], in_=gt.rearrange("(p t) o -> p (t o)", t=PACK))
+        n1_sb = lists.tile([P, H // 16], U16, name="n1_sb")
+        nc.sync.dma_start(n1_sb[:], n1)
+        n2_sb = lists.tile([P, H // 16], U16, name="n2_sb")
+        nc.sync.dma_start(n2_sb[:], n2)
+        w1_raw = keep.tile([P, PACK, N], F32, name="w1_raw")
+        nc.sync.dma_start(out=w1_raw[:], in_=w1.rearrange("(p t) w -> p t w", t=PACK))
+        n3_sb = lists.tile([P, W // 16], U16, name="n3_sb")
+        nc.sync.dma_start(n3_sb[:], n3)
+        n4_sb = lists.tile([P, W // 16], U16, name="n4_sb")
+        nc.sync.dma_start(n4_sb[:], n4)
+
+        picked_scales = keep.tile([P, S], U8, name="picked_scales")
+        nc.vector.tensor_copy(picked_scales[:], table_scales[:].indirect(offs_sb[:]))
+        x_sc = keep.tile([P, S], U8, align_bytes=64, name="x_sc")
+        nc.vector.tensor_copy(
+            out=x_sc[:].rearrange("p (t m) -> p t m", t=PACK),
+            in_=picked_scales[:].rearrange("p (m t) -> p t m", t=PACK),
+        )
+        picked_words = keep.tile([P, S], U32, name="picked_words")
+        nc.vector.tensor_copy(picked_words[:], table_words[:].indirect(offs_sb[:]))
+        x_codes = keep.tile([P, S], U32, align_bytes=64, name="x_codes")
+        nc.vector.tensor_copy(
+            out=x_codes[:].rearrange("p (t m) -> p t m", t=PACK),
+            in_=picked_words[:].rearrange("p (m t) -> p t m", t=PACK),
+        )
+
+        twice = keep.tile([P, PACK], F32, name="twice")
+        nc.gpsimd.tensor_scalar(twice[:], gate[:], 0.0, 2.0, ALU.is_ge, ALU.mult)
+        sign = keep.tile([P, PACK], F32, name="sign")
+        nc.gpsimd.tensor_scalar(sign[:], twice[:], 1.0, -1.0, ALU.mult, ALU.add)
+        size = keep.tile([P, PACK], F32, name="size")
+        nc.gpsimd.tensor_tensor(size[:], gate[:], sign[:], ALU.mult)
+
+        wa_q = []
+        for f in range(2):
+            grouped = keep.tile([P, HALF, PACK], BF16, align_bytes=64, name="wa_grouped%d" % f)
+            cut = HALF if f == 0 else 96
+            nc.scalar.copy(out=packed_view(grouped[:, :cut, :]), in_=planes_view(wa_raw[f][:, :, :cut]))
+            if cut < HALF:
+                nc.vector.tensor_copy(out=packed_view(grouped[:, cut:, :]), in_=planes_view(wa_raw[f][:, :, cut:]))
+            wa_q.append(quantise(grouped, HALF, "wa%d" % f))
+        y = [keep.tile([P, H], F32, name="y%d" % t) for t in range(PACK)]
+        y_acc = {}
+        for t in range(PACK):
+            rows = slice(t * P, (t + 1) * P)
+            for f in range(2):
+                cols = slice(f * HALF, (f + 1) * HALF)
+                acc = psum.tile([P, HALF], F32, name="bank%d_%d" % (f, t))
+                nc.tensor.matmul_mx(
+                    out=acc[:],
+                    lhsT=x_codes[:, rows].bitcast(FP8X4),
+                    lhsT_scale=x_sc[:, rows],
+                    rhs=wa_q[f][0][:].bitcast(FP8X4),
+                    rhs_scale=wa_q[f][1][:],
+                    start=True,
+                    stop=True,
+                )
+                y_acc[f, t] = acc
+                if f == 1:
+                    nc.vector.tensor_scalar(y[t][:, cols], acc[:], size[:, t : t + 1], None, ALU.mult)
+                else:
+                    nc.scalar.activation(y[t][:, cols], acc[:], ACT.Copy, scale=size[:, t : t + 1])
+
+        w1_grouped = []
+        for f in range(2):
+            grouped = keep.tile([P, HALF, PACK], BF16, align_bytes=64, name="w1_grouped%d" % f)
+            for r in range(2):
+                nc.gpsimd.tensor_tensor(
+                    packed_view(grouped[:, r * P : (r + 1) * P, :]),
+                    planes_view(w1_raw[:, :, f * HALF + r * P : f * HALF + (r + 1) * P]),
+                    sign[:].unsqueeze(1).unsqueeze(3).to_broadcast([P, P // RUN, PACK, RUN]),
+                    ALU.mult,
+                )
+            w1_grouped.append(grouped)
+
+        z = []
+        w1_q = []
+        for f in range(2):
+            entries = slice(f * HALF // 16, (f + 1) * HALF // 16)
+            first = keep.tile([P, PACK, HALF], F32, name="first%d" % f)
+            second = keep.tile([P, PACK, HALF], F32, name="second%d" % f)
+            larger = keep.tile([P, PACK, HALF], F32, name="larger%d" % f)
+            for t in range(PACK):
+                nc.scalar.activation(first[:, t, :], y[t][:].indirect(n1_sb[:, entries]), ACT.Copy)
+            for t in range(PACK):
+                if f * PACK + t < 4:
+                    nc.vector.tensor_copy(second[:, t, :], y[t][:].indirect(n2_sb[:, entries]))
+                else:
+                    nc.scalar.activation(second[:, t, :], y[t][:].indirect(n2_sb[:, entries]), ACT.Copy)
+            for t in range(PACK):
+                nc.vector.scalar_tensor_tensor(
+                    larger[:, t, :], y_acc[f, t][:], size[:, t : t + 1], first[:, t, :], ALU.mult, ALU.max
+                )
+            if f == 1:
+                w1_q.append(quantise(w1_grouped[0], HALF, "w1_0"))
+            name = "z_grouped0" if f == 0 else "w1_grouped0"
+            grouped = keep.tile([P, HALF, PACK], BF16, align_bytes=64, name=name)
+            nc.vector.tensor_tensor(packed_view(grouped[:]), planes_view(larger[:]), planes_view(second[:]), ALU.min)
+            z.append(quantise(grouped, HALF, "z%d" % f))
+        w1_q.append(quantise(w1_grouped[1], HALF, "w1_1"))
+
+        tiles = range(N // P)
+        lower = slice(0, HALF)
+        upper = slice(HALF, H)
+        by_table = N // P - 0
+        h = [keep.tile([P, H], F32, name="h%d" % r) for r in tiles]
+        mag = [keep.tile([P, H], F32, name="mag%d" % r) for r in range(2)]
+        h_acc = {}
+        for f in range(2):
+            for r in tiles:
+                rows = slice(r % 2 * P, (r % 2 + 1) * P)
+                acc = psum.tile([P, HALF], F32, name="bank%d_%d" % (f, r))
+                nc.tensor.matmul_mx(
+                    out=acc[:],
+                    lhsT=w1_q[r // 2][0][:, rows].bitcast(FP8X4),
+                    lhsT_scale=w1_q[r // 2][1][:, rows],
+                    rhs=z[f][0][:].bitcast(FP8X4),
+                    rhs_scale=z[f][1][:],
+                    start=True,
+                    stop=True,
+                )
+                h_acc[f, r] = acc
+                if f == 0 and r < 2:
+                    nc.scalar.copy(h[r][:, lower], acc[:])
+                    if r < min(by_table, 2):
+                        nc.scalar.activation(mag[r][:, lower], acc[:], ACT.Abs)
+        old = [keep.tile([P, W], F32, name="old%d" % r) for r in tiles]
+        pa = [keep.tile([P, W], F32, name="pa%d" % r) for r in tiles]
+        ra = [keep.tile([P, W], F32, name="ra%d" % r) for r in tiles]
+
+        def fetch(r):
+            if r == 0:
+                nc.scalar.copy(h[r][:, upper], h_acc[1, r][:])
+            else:
+                if r >= 2:
+                    nc.vector.tensor_copy(h[r][:, lower], h_acc[0, r][:])
+                nc.vector.tensor_copy(h[r][:, upper], h_acc[1, r][:])
+            nc.scalar.activation(old[r][:], h[r][:].indirect(n3_sb[:]), ACT.Copy)
+
+        def fetch_sizes(r):
+            if r < by_table and r < 2:
+                nc.vector.scalar_tensor_tensor(
+                    mag[r][:, upper], h_acc[1, r][:], -1.0, h[r][:, upper], ALU.mult, ALU.max
+                )
+                nc.vector.tensor_copy(pa[r][:], mag[r][:].indirect(n4_sb[:]))
+            else:
+                signed = keep.tile([P, W], F32, name="signed%d" % r)
+                nc.vector.tensor_copy(signed[:], h[r][:].indirect(n4_sb[:]))
+                nc.vector.scalar_tensor_tensor(pa[r][:], signed[:], -1.0, signed[:], ALU.mult, ALU.max)
+
+        root = [keep.tile([P, W], F32, name="root%d" % r) for r in tiles]
+
+        def invert(r):
+            nc.scalar.activation(root[r][:], pa[r][:], ACT.Abs_reciprocal_sqrt, bias=0.5)
+
+        def multiply(r):
+            part = keep.tile([P, W], F32, name="part%d" % r)
+            nc.vector.tensor_tensor(part[:], old[r][:], root[r][:], ALU.mult)
+            nc.vector.tensor_tensor(ra[r][:], part[:], root[r][:], ALU.mult)
+
+        def put(r):
+            nc.scalar.activation(h[r][:].indirect(n3_sb[:]), ra[r][:], ACT.Copy)
+            nc.sync.dma_start(out=out[r * P : (r + 1) * P, :], in_=h[r][:])
+
+        fetch(0)
+        fetch(1)
+        fetch_sizes(0)
+        fetch(2)
+        invert(0)
+        fetch_sizes(1)
+        invert(1)
+        fetch(3)
+        multiply(0)
+        put(0)
+        fetch_sizes(2)
+        invert(2)
+        multiply(1)
+        put(1)
+        fetch_sizes(3)
+        invert(3)
+        multiply(2)
+        put(2)
+        multiply(3)
+        put(3)

@@ -19,6 +19,7 @@ P = 128
 PACK = 4
 HALF = H // 2
 RUN = 4
+PIECES = (256, 256)
 
 
 def packed_view(tile):
@@ -49,6 +50,8 @@ def tile_picked_tokminmxknorm_none_p_kernel(
         wa_rows = wa.rearrange("(p t) w -> p t w", t=PACK)
         wa_raw = [keep.tile([P, PACK, HALF], F32, name="wa_raw%d" % f) for f in range(2)]
         nc.sync.dma_start(out=wa_raw[0][:], in_=wa_rows[:, :, 0:HALF])
+        offs_sb = lists.tile([P, S // 16], U16, name="offs_sb")
+        nc.sync.dma_start(offs_sb[:], offs)
         table_scales = keep.tile([P, T], U8, name="table_scales")
         nc.gpsimd.memset(table_scales[:].bitcast(I32), 0)
         for q in range(4):
@@ -56,15 +59,13 @@ def tile_picked_tokminmxknorm_none_p_kernel(
                 out=table_scales[32 * q : 32 * q + 4, :].bitcast(I32),
                 in_=x_scales[0, 4 * q : 4 * q + 4, :].bitcast(I32),
             )
-        offs_sb = lists.tile([P, S // 16], U16, name="offs_sb")
-        nc.sync.dma_start(offs_sb[:], offs)
         table_words = keep.tile([P, T], U32, name="table_words")
         nc.sync.dma_start(
             out=table_words[:].bitcast(I32), in_=x_words[0].rearrange("p n t -> p (n t)").bitcast(I32)
         )
         nc.sync.dma_start(out=wa_raw[1][:], in_=wa_rows[:, :, HALF:H])
         gate = keep.tile([P, PACK], F32, name="gate")
-        nc.sync.dma_start(out=gate[:], in_=gt.rearrange("(p t) o -> p (t o)", t=PACK))
+        nc.gpsimd.dma_start(out=gate[:], in_=gt.rearrange("(p t) o -> p (t o)", t=PACK))
         n1_sb = lists.tile([P, H // 16], U16, name="n1_sb")
         nc.sync.dma_start(n1_sb[:], n1)
         n2_sb = lists.tile([P, H // 16], U16, name="n2_sb")
@@ -98,6 +99,8 @@ def tile_picked_tokminmxknorm_none_p_kernel(
         size = keep.tile([P, PACK], F32, name="size")
         nc.gpsimd.tensor_tensor(size[:], gate[:], sign[:], ALU.mult)
 
+        warm = keep.tile([P, 1], F32, name="warm")
+        nc.scalar.activation(warm[:], wa_raw[0][:, 0, 0:1], ACT.Abs_reciprocal_sqrt, bias=0.5, scale=0.0)
         wa_q = []
         for f in range(2):
             grouped = keep.tile([P, HALF, PACK], BF16, align_bytes=64, name="wa_grouped%d" % f)
@@ -128,90 +131,91 @@ def tile_picked_tokminmxknorm_none_p_kernel(
                 else:
                     nc.scalar.activation(y[t][:, cols], acc[:], ACT.Copy, scale=size[:, t : t + 1])
 
-        w1_grouped = []
-        for f in range(2):
-            grouped = keep.tile([P, HALF, PACK], BF16, align_bytes=64, name="w1_grouped%d" % f)
-            for r in range(2):
-                nc.gpsimd.tensor_tensor(
-                    packed_view(grouped[:, r * P : (r + 1) * P, :]),
-                    planes_view(w1_raw[:, :, f * HALF + r * P : f * HALF + (r + 1) * P]),
-                    sign[:].unsqueeze(1).unsqueeze(3).to_broadcast([P, P // RUN, PACK, RUN]),
-                    ALU.mult,
-                )
-            w1_grouped.append(grouped)
+        w1_grouped = keep.tile([P, N, PACK], BF16, align_bytes=64, name="w1_grouped")
+        for r in range(N // P):
+            nc.gpsimd.tensor_tensor(
+                packed_view(w1_grouped[:, r * P : (r + 1) * P, :]),
+                planes_view(w1_raw[:, :, r * P : (r + 1) * P]),
+                sign[:].unsqueeze(1).unsqueeze(3).to_broadcast([P, P // RUN, PACK, RUN]),
+                ALU.mult,
+            )
 
         z = []
-        w1_q = []
-        for f in range(2):
-            entries = slice(f * HALF // 16, (f + 1) * HALF // 16)
-            first = keep.tile([P, PACK, HALF], F32, name="first%d" % f)
-            second = keep.tile([P, PACK, HALF], F32, name="second%d" % f)
-            larger = keep.tile([P, PACK, HALF], F32, name="larger%d" % f)
+        start = 0
+        for f, width in enumerate(PIECES):
+            entries = slice(start // 16, (start + width) // 16)
+            half, inside = divmod(start, HALF)
+            first = keep.tile([P, PACK, width], F32, name="first%d" % f)
+            second = keep.tile([P, PACK, width], F32, name="second%d" % f)
+            larger = keep.tile([P, PACK, width], F32, name="larger%d" % f)
             for t in range(PACK):
                 nc.scalar.activation(first[:, t, :], y[t][:].indirect(n1_sb[:, entries]), ACT.Copy)
             for t in range(PACK):
-                if f * PACK + t < 4:
+                if f == 0 and t < 3:
                     nc.vector.tensor_copy(second[:, t, :], y[t][:].indirect(n2_sb[:, entries]))
                 else:
                     nc.scalar.activation(second[:, t, :], y[t][:].indirect(n2_sb[:, entries]), ACT.Copy)
             for t in range(PACK):
                 nc.vector.scalar_tensor_tensor(
-                    larger[:, t, :], y_acc[f, t][:], size[:, t : t + 1], first[:, t, :], ALU.mult, ALU.max
+                    larger[:, t, :],
+                    y_acc[half, t][:, inside : inside + width],
+                    size[:, t : t + 1],
+                    first[:, t, :],
+                    ALU.mult,
+                    ALU.max,
                 )
             if f == 1:
-                w1_q.append(quantise(w1_grouped[0], HALF, "w1_0"))
-            name = "z_grouped0" if f == 0 else "w1_grouped0"
-            grouped = keep.tile([P, HALF, PACK], BF16, align_bytes=64, name=name)
+                w1_codes, w1_scales = quantise(w1_grouped, N, "w1")
+            name = "w1_grouped" if f == 1 else "z_grouped%d" % f
+            grouped = keep.tile([P, width, PACK], BF16, align_bytes=64, name=name)
             nc.vector.tensor_tensor(packed_view(grouped[:]), planes_view(larger[:]), planes_view(second[:]), ALU.min)
-            z.append(quantise(grouped, HALF, "z%d" % f))
-        w1_q.append(quantise(w1_grouped[1], HALF, "w1_1"))
+            z.append(quantise(grouped, width, "z%d" % f))
+            start = start + width
 
         tiles = range(N // P)
         lower = slice(0, HALF)
         upper = slice(HALF, H)
-        by_table = N // P - 0
+        by_table = N // P
         h = [keep.tile([P, H], F32, name="h%d" % r) for r in tiles]
-        mag = [keep.tile([P, H], F32, name="mag%d" % r) for r in range(2)]
+        mag = [keep.tile([P, H], F32, name="mag%d" % r) for r in range(0)]
         h_acc = {}
-        for f in range(2):
+        start = 0
+        for f, width in enumerate(PIECES):
+            half, inside = divmod(start, HALF)
             for r in tiles:
-                rows = slice(r % 2 * P, (r % 2 + 1) * P)
-                acc = psum.tile([P, HALF], F32, name="bank%d_%d" % (f, r))
+                rows = slice(r * P, (r + 1) * P)
+                if inside == 0:
+                    h_acc[half, r] = psum.tile([P, HALF], F32, name="bank%d_%d" % (half, r))
                 nc.tensor.matmul_mx(
-                    out=acc[:],
-                    lhsT=w1_q[r // 2][0][:, rows].bitcast(FP8X4),
-                    lhsT_scale=w1_q[r // 2][1][:, rows],
+                    out=h_acc[half, r][:, inside : inside + width],
+                    lhsT=w1_codes[:, rows].bitcast(FP8X4),
+                    lhsT_scale=w1_scales[:, rows],
                     rhs=z[f][0][:].bitcast(FP8X4),
                     rhs_scale=z[f][1][:],
                     start=True,
                     stop=True,
                 )
-                h_acc[f, r] = acc
-                if f == 0 and r < 2:
-                    nc.scalar.copy(h[r][:, lower], acc[:])
-                    if r < min(by_table, 2):
-                        nc.scalar.activation(mag[r][:, lower], acc[:], ACT.Abs)
+                if f == 0 and r < 4:
+                    nc.scalar.copy(h[r][:, lower], h_acc[0, r][:])
+            start = start + width
+        for r in range(0):
+            nc.scalar.activation(mag[r][:, lower], h_acc[0, r][:], ACT.Abs)
         old = [keep.tile([P, W], F32, name="old%d" % r) for r in tiles]
         pa = [keep.tile([P, W], F32, name="pa%d" % r) for r in tiles]
-        ra = [keep.tile([P, W], F32, name="ra%d" % r) for r in tiles]
+        ra = {}
 
         def fetch(r):
-            if r == 0:
-                nc.scalar.copy(h[r][:, upper], h_acc[1, r][:])
-            else:
-                if r >= 2:
-                    nc.vector.tensor_copy(h[r][:, lower], h_acc[0, r][:])
-                nc.vector.tensor_copy(h[r][:, upper], h_acc[1, r][:])
+            nc.vector.tensor_copy(h[r][:, upper], h_acc[1, r][:])
             nc.scalar.activation(old[r][:], h[r][:].indirect(n3_sb[:]), ACT.Copy)
 
         def fetch_sizes(r):
-            if r < by_table and r < 2:
+            if r < 0:
                 nc.vector.scalar_tensor_tensor(
                     mag[r][:, upper], h_acc[1, r][:], -1.0, h[r][:, upper], ALU.mult, ALU.max
                 )
                 nc.vector.tensor_copy(pa[r][:], mag[r][:].indirect(n4_sb[:]))
             else:
-                signed = keep.tile([P, W], F32, name="signed%d" % r)
+                signed = keep.tile([P, W], F32, name="signed1" if r < 2 else "part%d" % (r - 2))
                 nc.vector.tensor_copy(signed[:], h[r][:].indirect(n4_sb[:]))
                 nc.vector.scalar_tensor_tensor(pa[r][:], signed[:], -1.0, signed[:], ALU.mult, ALU.max)
 
@@ -222,8 +226,12 @@ def tile_picked_tokminmxknorm_none_p_kernel(
 
         def multiply(r):
             part = keep.tile([P, W], F32, name="part%d" % r)
-            nc.vector.tensor_tensor(part[:], old[r][:], root[r][:], ALU.mult)
-            nc.vector.tensor_tensor(ra[r][:], part[:], root[r][:], ALU.mult)
+            ra[r] = keep.tile([P, W], F32, name="signed1" if r == 0 else "part%d" % (r - 1))
+            step = W // 2 if r < 1 else W
+            for a in range(0, W, step):
+                nc.vector.tensor_tensor(part[:, a : a + step], old[r][:, a : a + step], root[r][:, a : a + step], ALU.mult)
+            for a in range(0, W, step):
+                nc.vector.tensor_tensor(ra[r][:, a : a + step], part[:, a : a + step], root[r][:, a : a + step], ALU.mult)
 
         def put(r):
             nc.scalar.activation(h[r][:].indirect(n3_sb[:]), ra[r][:], ACT.Copy)

@@ -19,11 +19,12 @@ P = 128
 PACK = 4
 HALF = H // 2
 RUN = 4
-PIECES = (256, 256)
+WIDE = 256
+PIECES = (slice(0, WIDE), slice(WIDE, H))
 
 
-def packed_view(tile):
-    return tile.rearrange("p (c i) t -> p c t i", i=RUN)
+def packed_view(ap):
+    return ap.rearrange("p (c i) t -> p c t i", i=RUN)
 
 
 def planes_view(ap):
@@ -47,11 +48,24 @@ def tile_picked_tokminmxknorm_none_p_kernel(
             )
             return codes, scales
 
+        def product(acc, left, rows, right, cols):
+            nc.tensor.matmul_mx(
+                out=acc,
+                lhsT=left[0][:, rows].bitcast(FP8X4),
+                lhsT_scale=left[1][:, rows],
+                rhs=right[0][:, cols].bitcast(FP8X4),
+                rhs_scale=right[1][:, cols],
+                start=True,
+                stop=True,
+            )
+
         wa_rows = wa.rearrange("(p t) w -> p t w", t=PACK)
         wa_raw = [keep.tile([P, PACK, HALF], F32, name="wa_raw%d" % f) for f in range(2)]
-        nc.sync.dma_start(out=wa_raw[0][:], in_=wa_rows[:, :, 0:HALF])
+        nc.sync.dma_start(out=wa_raw[0][:], in_=wa_rows[:, :, :HALF])
         offs_sb = lists.tile([P, S // 16], U16, name="offs_sb")
         nc.sync.dma_start(offs_sb[:], offs)
+        n1_sb = lists.tile([P, H // 16], U16, name="n1_sb")
+        nc.sync.dma_start(n1_sb[:], n1)
         table_scales = keep.tile([P, T], U8, name="table_scales")
         nc.gpsimd.memset(table_scales[:].bitcast(I32), 0)
         for q in range(4):
@@ -63,11 +77,9 @@ def tile_picked_tokminmxknorm_none_p_kernel(
         nc.sync.dma_start(
             out=table_words[:].bitcast(I32), in_=x_words[0].rearrange("p n t -> p (n t)").bitcast(I32)
         )
-        nc.sync.dma_start(out=wa_raw[1][:], in_=wa_rows[:, :, HALF:H])
+        nc.sync.dma_start(out=wa_raw[1][:], in_=wa_rows[:, :, HALF:])
         gate = keep.tile([P, PACK], F32, name="gate")
         nc.gpsimd.dma_start(out=gate[:], in_=gt.rearrange("(p t) o -> p (t o)", t=PACK))
-        n1_sb = lists.tile([P, H // 16], U16, name="n1_sb")
-        nc.sync.dma_start(n1_sb[:], n1)
         n2_sb = lists.tile([P, H // 16], U16, name="n2_sb")
         nc.sync.dma_start(n2_sb[:], n2)
         w1_raw = keep.tile([P, PACK, N], F32, name="w1_raw")
@@ -76,21 +88,6 @@ def tile_picked_tokminmxknorm_none_p_kernel(
         nc.sync.dma_start(n3_sb[:], n3)
         n4_sb = lists.tile([P, W // 16], U16, name="n4_sb")
         nc.sync.dma_start(n4_sb[:], n4)
-
-        picked_scales = keep.tile([P, S], U8, name="picked_scales")
-        nc.vector.tensor_copy(picked_scales[:], table_scales[:].indirect(offs_sb[:]))
-        x_sc = keep.tile([P, S], U8, align_bytes=64, name="x_sc")
-        nc.vector.tensor_copy(
-            out=x_sc[:].rearrange("p (t m) -> p t m", t=PACK),
-            in_=picked_scales[:].rearrange("p (m t) -> p t m", t=PACK),
-        )
-        picked_words = keep.tile([P, S], U32, name="picked_words")
-        nc.vector.tensor_copy(picked_words[:], table_words[:].indirect(offs_sb[:]))
-        x_codes = keep.tile([P, S], U32, align_bytes=64, name="x_codes")
-        nc.vector.tensor_copy(
-            out=x_codes[:].rearrange("p (t m) -> p t m", t=PACK),
-            in_=picked_words[:].rearrange("p (m t) -> p t m", t=PACK),
-        )
 
         twice = keep.tile([P, PACK], F32, name="twice")
         nc.gpsimd.tensor_scalar(twice[:], gate[:], 0.0, 2.0, ALU.is_ge, ALU.mult)
@@ -101,39 +98,55 @@ def tile_picked_tokminmxknorm_none_p_kernel(
 
         warm = keep.tile([P, 1], F32, name="warm")
         nc.scalar.activation(warm[:], wa_raw[0][:, 0, 0:1], ACT.Abs_reciprocal_sqrt, bias=0.5, scale=0.0)
-        wa_q = []
-        for f in range(2):
+        picked_scales = keep.tile([P, S], U8, align_bytes=64, name="picked_scales")
+        nc.vector.tensor_copy(picked_scales[:], table_scales[:].indirect(offs_sb[:]))
+        x_scale = keep.tile([P, S], U8, align_bytes=64, name="x_scale")
+        nc.vector.tensor_copy(
+            out=x_scale[:].rearrange("p (t m) -> p t m", t=PACK),
+            in_=picked_scales[:].rearrange("p (m t) -> p t m", t=PACK),
+        )
+        wa_codes = keep.tile([P, H], U32, align_bytes=64, name="wa_codes")
+        wa_scales = keep.tile([P, H], U8, align_bytes=64, name="picked_scales")
+
+        def quantise_wa(f, cut):
+            cols = slice(f * HALF, (f + 1) * HALF)
             grouped = keep.tile([P, HALF, PACK], BF16, align_bytes=64, name="wa_grouped%d" % f)
-            cut = HALF if f == 0 else 96
             nc.scalar.copy(out=packed_view(grouped[:, :cut, :]), in_=planes_view(wa_raw[f][:, :, :cut]))
             if cut < HALF:
                 nc.vector.tensor_copy(out=packed_view(grouped[:, cut:, :]), in_=planes_view(wa_raw[f][:, :, cut:]))
-            wa_q.append(quantise(grouped, HALF, "wa%d" % f))
+            nc.vector.quantize_mx(
+                out=wa_codes[:, cols].bitcast(FP8X4),
+                scales=wa_scales[:, cols],
+                in_=grouped[:].rearrange("p c t -> p (c t)"),
+            )
+
+        quantise_wa(0, HALF)
+        picked_words = keep.tile([P, S], U32, name="picked_words")
+        nc.vector.tensor_copy(picked_words[:], table_words[:].indirect(offs_sb[:]))
+        x_codes = keep.tile([P, S], U32, align_bytes=64, name="x_codes")
+        nc.vector.tensor_copy(
+            out=x_codes[:].rearrange("p (t m) -> p m t", t=PACK),
+            in_=picked_words[:].rearrange("p (m t) -> p m t", t=PACK),
+        )
+        quantise_wa(1, 128)
+
         y = [keep.tile([P, H], F32, name="y%d" % t) for t in range(PACK)]
         y_acc = {}
         for t in range(PACK):
-            rows = slice(t * P, (t + 1) * P)
             for f in range(2):
                 cols = slice(f * HALF, (f + 1) * HALF)
                 acc = psum.tile([P, HALF], F32, name="bank%d_%d" % (f, t))
-                nc.tensor.matmul_mx(
-                    out=acc[:],
-                    lhsT=x_codes[:, rows].bitcast(FP8X4),
-                    lhsT_scale=x_sc[:, rows],
-                    rhs=wa_q[f][0][:].bitcast(FP8X4),
-                    rhs_scale=wa_q[f][1][:],
-                    start=True,
-                    stop=True,
-                )
+                product(acc[:], (x_codes, x_scale), slice(t * P, (t + 1) * P), (wa_codes, wa_scales), cols)
                 y_acc[f, t] = acc
-                if f == 1:
+                if f == 1 and t % 2 == 0:
                     nc.vector.tensor_scalar(y[t][:, cols], acc[:], size[:, t : t + 1], None, ALU.mult)
                 else:
                     nc.scalar.activation(y[t][:, cols], acc[:], ACT.Copy, scale=size[:, t : t + 1])
 
         w1_grouped = keep.tile([P, N, PACK], BF16, align_bytes=64, name="w1_grouped")
         for r in range(N // P):
-            nc.gpsimd.tensor_tensor(
+            engine = nc.gpsimd if r < 4 else nc.vector
+            engine.tensor_tensor(
                 packed_view(w1_grouped[:, r * P : (r + 1) * P, :]),
                 planes_view(w1_raw[:, :, r * P : (r + 1) * P]),
                 sign[:].unsqueeze(1).unsqueeze(3).to_broadcast([P, P // RUN, PACK, RUN]),
@@ -141,97 +154,86 @@ def tile_picked_tokminmxknorm_none_p_kernel(
             )
 
         z = []
-        start = 0
-        for f, width in enumerate(PIECES):
-            entries = slice(start // 16, (start + width) // 16)
-            half, inside = divmod(start, HALF)
+        for f, cols in enumerate(PIECES):
+            width = cols.stop - cols.start
+            entries = slice(cols.start // 16, cols.stop // 16)
             first = keep.tile([P, PACK, width], F32, name="first%d" % f)
             second = keep.tile([P, PACK, width], F32, name="second%d" % f)
             larger = keep.tile([P, PACK, width], F32, name="larger%d" % f)
             for t in range(PACK):
                 nc.scalar.activation(first[:, t, :], y[t][:].indirect(n1_sb[:, entries]), ACT.Copy)
             for t in range(PACK):
-                if f == 0 and t < 3:
+                if f * PACK + t < 4:
                     nc.vector.tensor_copy(second[:, t, :], y[t][:].indirect(n2_sb[:, entries]))
                 else:
                     nc.scalar.activation(second[:, t, :], y[t][:].indirect(n2_sb[:, entries]), ACT.Copy)
             for t in range(PACK):
-                nc.vector.scalar_tensor_tensor(
-                    larger[:, t, :],
-                    y_acc[half, t][:, inside : inside + width],
-                    size[:, t : t + 1],
-                    first[:, t, :],
-                    ALU.mult,
-                    ALU.max,
-                )
+                for half in range(2):
+                    lo, hi = max(cols.start, half * HALF), min(cols.stop, (half + 1) * HALF)
+                    if lo < hi:
+                        nc.vector.scalar_tensor_tensor(
+                            larger[:, t, lo - cols.start : hi - cols.start],
+                            y_acc[half, t][:, lo - half * HALF : hi - half * HALF],
+                            size[:, t : t + 1],
+                            first[:, t, lo - cols.start : hi - cols.start],
+                            ALU.mult,
+                            ALU.max,
+                        )
             if f == 1:
-                w1_codes, w1_scales = quantise(w1_grouped, N, "w1")
-            name = "w1_grouped" if f == 1 else "z_grouped%d" % f
+                w1_q = quantise(w1_grouped, N, "w1")
+            name = "w1_grouped" if f == 1 else "z_grouped"
             grouped = keep.tile([P, width, PACK], BF16, align_bytes=64, name=name)
             nc.vector.tensor_tensor(packed_view(grouped[:]), planes_view(larger[:]), planes_view(second[:]), ALU.min)
             z.append(quantise(grouped, width, "z%d" % f))
-            start = start + width
 
         tiles = range(N // P)
-        lower = slice(0, HALF)
-        upper = slice(HALF, H)
-        by_table = N // P
         h = [keep.tile([P, H], F32, name="h%d" % r) for r in tiles]
-        mag = [keep.tile([P, H], F32, name="mag%d" % r) for r in range(0)]
         h_acc = {}
-        start = 0
-        for f, width in enumerate(PIECES):
-            half, inside = divmod(start, HALF)
+        for f, cols in enumerate(PIECES):
+            width = cols.stop - cols.start
             for r in tiles:
-                rows = slice(r * P, (r + 1) * P)
-                if inside == 0:
-                    h_acc[half, r] = psum.tile([P, HALF], F32, name="bank%d_%d" % (half, r))
-                nc.tensor.matmul_mx(
-                    out=h_acc[half, r][:, inside : inside + width],
-                    lhsT=w1_codes[:, rows].bitcast(FP8X4),
-                    lhsT_scale=w1_scales[:, rows],
-                    rhs=z[f][0][:].bitcast(FP8X4),
-                    rhs_scale=z[f][1][:],
-                    start=True,
-                    stop=True,
-                )
+                h_acc[f, r] = psum.tile([P, width], F32, name="bank%d_%d" % (f, r))
+                for a in range(0, width, HALF):
+                    part = slice(a, min(a + HALF, width))
+                    product(h_acc[f, r][:, part], w1_q, slice(r * P, (r + 1) * P), z[f], part)
                 if f == 0 and r < 4:
-                    nc.scalar.copy(h[r][:, lower], h_acc[0, r][:])
-            start = start + width
-        for r in range(0):
-            nc.scalar.activation(mag[r][:, lower], h_acc[0, r][:], ACT.Abs)
+                    nc.scalar.copy(h[r][:, cols], h_acc[f, r][:])
         old = [keep.tile([P, W], F32, name="old%d" % r) for r in tiles]
         pa = [keep.tile([P, W], F32, name="pa%d" % r) for r in tiles]
+        root = [keep.tile([P, W], F32, name="root%d" % r) for r in tiles]
         ra = {}
 
         def fetch(r):
-            nc.vector.tensor_copy(h[r][:, upper], h_acc[1, r][:])
+            if r >= 4:
+                nc.vector.tensor_copy(h[r][:, PIECES[0]], h_acc[0, r][:])
+            nc.vector.tensor_copy(h[r][:, PIECES[1]], h_acc[1, r][:])
             nc.scalar.activation(old[r][:], h[r][:].indirect(n3_sb[:]), ACT.Copy)
 
         def fetch_sizes(r):
-            if r < 0:
-                nc.vector.scalar_tensor_tensor(
-                    mag[r][:, upper], h_acc[1, r][:], -1.0, h[r][:, upper], ALU.mult, ALU.max
-                )
-                nc.vector.tensor_copy(pa[r][:], mag[r][:].indirect(n4_sb[:]))
-            else:
-                signed = keep.tile([P, W], F32, name="signed1" if r < 2 else "part%d" % (r - 2))
-                nc.vector.tensor_copy(signed[:], h[r][:].indirect(n4_sb[:]))
-                nc.vector.scalar_tensor_tensor(pa[r][:], signed[:], -1.0, signed[:], ALU.mult, ALU.max)
-
-        root = [keep.tile([P, W], F32, name="root%d" % r) for r in tiles]
+            signed = keep.tile([P, W], F32, name="signed" if r < 2 else "part%d" % (r - 2))
+            nc.vector.tensor_copy(signed[:], h[r][:].indirect(n4_sb[:]))
+            nc.vector.scalar_tensor_tensor(pa[r][:], signed[:], -1.0, signed[:], ALU.mult, ALU.max)
 
         def invert(r):
-            nc.scalar.activation(root[r][:], pa[r][:], ACT.Abs_reciprocal_sqrt, bias=0.5)
+            cut = W - 0 if r == 3 else W
+            if cut > 0:
+                nc.scalar.activation(root[r][:, :cut], pa[r][:, :cut], ACT.Abs_reciprocal_sqrt, bias=0.5)
 
         def multiply(r):
+            cut = W - 0 if r == 3 else W
             part = keep.tile([P, W], F32, name="part%d" % r)
-            ra[r] = keep.tile([P, W], F32, name="signed1" if r == 0 else "part%d" % (r - 1))
+            ra[r] = keep.tile([P, W], F32, name="signed" if r == 0 else "part%d" % (r - 1))
             step = W // 2 if r < 1 else W
-            for a in range(0, W, step):
-                nc.vector.tensor_tensor(part[:, a : a + step], old[r][:, a : a + step], root[r][:, a : a + step], ALU.mult)
-            for a in range(0, W, step):
-                nc.vector.tensor_tensor(ra[r][:, a : a + step], part[:, a : a + step], root[r][:, a : a + step], ALU.mult)
+            if cut < W:
+                nc.vector.tensor_scalar(part[:, cut:], pa[r][:, cut:], 0.5, None, ALU.add)
+                nc.vector.reciprocal(root[r][:, cut:], part[:, cut:])
+                nc.vector.tensor_tensor(ra[r][:, cut:], old[r][:, cut:], root[r][:, cut:], ALU.mult)
+            for a in range(0, cut, step):
+                b = min(a + step, cut)
+                nc.vector.tensor_tensor(part[:, a:b], old[r][:, a:b], root[r][:, a:b], ALU.mult)
+            for a in range(0, cut, step):
+                b = min(a + step, cut)
+                nc.vector.tensor_tensor(ra[r][:, a:b], part[:, a:b], root[r][:, a:b], ALU.mult)
 
         def put(r):
             nc.scalar.activation(h[r][:].indirect(n3_sb[:]), ra[r][:], ACT.Copy)

from contextlib import ExitStack

import concourse.mybir as mybir

K, T, S, N, H, W = 512, 2048, 512, 512, 512, 384
FLOPS = 2 * K * S * H + 2 * S * N * H

F32 = mybir.dt.float32
BF16 = mybir.dt.bfloat16
I32 = mybir.dt.int32
U32 = mybir.dt.uint32
U16 = mybir.dt.uint16
U8 = mybir.dt.uint8
FP8X4 = mybir.dt.float8_e4m3fn_x4
ALU = mybir.AluOpType
ACT = mybir.ActivationFunctionType

P = 128
PACK = 4
HALF = H // 2
RUN = 4
WIDE = 256
PIECES = (slice(0, WIDE), slice(WIDE, H))


def packed_view(ap):
    return ap.rearrange("p (c i) t -> p c t i", i=RUN)


def planes_view(ap):
    return ap.rearrange("p t (c i) -> p c t i", i=RUN)


def tile_picked_tokminmxknorm_none_p_kernel(
    tc, x_words, x_scales, wa, gt, w1, offs, n1, n2, n3, n4, out
):
    nc = tc.nc
    with ExitStack() as ctx:
        lists = ctx.enter_context(tc.tile_pool(name="lists", bufs=1))
        keep = ctx.enter_context(tc.tile_pool(name="keep", bufs=1))
        psum = ctx.enter_context(tc.psum_pool(name="psum", bufs=1))

        def quantise(grouped, width, name):
            codes = keep.tile([P, width], U32, align_bytes=64, name=name + "_codes")
            scales = keep.tile([P, width], U8, align_bytes=64, name=name + "_scales")
            nc.vector.quantize_mx(
                out=codes[:].bitcast(FP8X4), scales=scales[:], in_=grouped[:].rearrange("p c t -> p (c t)")
            )
            return codes, scales

        def product(acc, left, rows, right, cols):
            nc.tensor.matmul_mx(
                out=acc,
                lhsT=left[0][:, rows].bitcast(FP8X4),
                lhsT_scale=left[1][:, rows],
                rhs=right[0][:, cols].bitcast(FP8X4),
                rhs_scale=right[1][:, cols],
                start=True,
                stop=True,
            )

        wa_rows = wa.rearrange("(p t) w -> p t w", t=PACK)
        wa_raw = [keep.tile([P, PACK, HALF], F32, name="wa_raw%d" % f) for f in range(2)]
        nc.sync.dma_start(out=wa_raw[0][:], in_=wa_rows[:, :, :HALF])
        offs_sb = lists.tile([P, S // 16], U16, name="offs_sb")
        nc.sync.dma_start(offs_sb[:], offs)
        n1_sb = lists.tile([P, H // 16], U16, name="n1_sb")
        nc.sync.dma_start(n1_sb[:], n1)
        table_scales = keep.tile([P, T], U8, name="table_scales")
        nc.gpsimd.memset(table_scales[:].bitcast(I32), 0)
        for q in range(4):
            nc.sync.dma_start(
                out=table_scales[32 * q : 32 * q + 4, :].bitcast(I32),
                in_=x_scales[0, 4 * q : 4 * q + 4, :].bitcast(I32),
            )
        table_words = keep.tile([P, T], U32, name="table_words")
        nc.sync.dma_start(
            out=table_words[:].bitcast(I32), in_=x_words[0].rearrange("p n t -> p (n t)").bitcast(I32)
        )
        nc.sync.dma_start(out=wa_raw[1][:], in_=wa_rows[:, :, HALF:])
        gate = keep.tile([P, PACK], F32, name="gate")
        nc.gpsimd.dma_start(out=gate[:], in_=gt.rearrange("(p t) o -> p (t o)", t=PACK))
        n2_sb = lists.tile([P, H // 16], U16, name="n2_sb")
        nc.sync.dma_start(n2_sb[:], n2)
        w1_raw = keep.tile([P, PACK, N], F32, name="w1_raw")
        nc.sync.dma_start(out=w1_raw[:], in_=w1.rearrange("(p t) w -> p t w", t=PACK))
        n3_sb = lists.tile([P, W // 16], U16, name="n3_sb")
        nc.sync.dma_start(n3_sb[:], n3)
        n4_sb = lists.tile([P, W // 16], U16, name="n4_sb")
        nc.sync.dma_start(n4_sb[:], n4)

        twice = keep.tile([P, PACK], F32, name="twice")
        nc.gpsimd.tensor_scalar(twice[:], gate[:], 0.0, 2.0, ALU.is_ge, ALU.mult)
        sign = keep.tile([P, PACK], F32, name="sign")
        nc.gpsimd.tensor_scalar(sign[:], twice[:], 1.0, -1.0, ALU.mult, ALU.add)
        size = keep.tile([P, PACK], F32, name="size")
        nc.gpsimd.tensor_tensor(size[:], gate[:], sign[:], ALU.mult)

        warm = keep.tile([P, 1], F32, name="warm")
        nc.scalar.activation(warm[:], wa_raw[0][:, 0, 0:1], ACT.Abs_reciprocal_sqrt, bias=0.5, scale=0.0)
        picked_scales = keep.tile([P, S], U8, align_bytes=64, name="picked_scales")
        nc.vector.tensor_copy(picked_scales[:], table_scales[:].indirect(offs_sb[:]))
        x_scale = keep.tile([P, S], U8, align_bytes=64, name="x_scale")
        nc.vector.tensor_copy(
            out=x_scale[:].rearrange("p (t m) -> p t m", t=PACK),
            in_=picked_scales[:].rearrange("p (m t) -> p t m", t=PACK),
        )
        wa_codes = keep.tile([P, H], U32, align_bytes=64, name="wa_codes")
        wa_scales = keep.tile([P, H], U8, align_bytes=64, name="picked_scales")

        def quantise_wa(f, cut):
            cols = slice(f * HALF, (f + 1) * HALF)
            grouped = keep.tile([P, HALF, PACK], BF16, align_bytes=64, name="wa_grouped%d" % f)
            nc.scalar.copy(out=packed_view(grouped[:, :cut, :]), in_=planes_view(wa_raw[f][:, :, :cut]))
            if cut < HALF:
                nc.vector.tensor_copy(out=packed_view(grouped[:, cut:, :]), in_=planes_view(wa_raw[f][:, :, cut:]))
            nc.vector.quantize_mx(
                out=wa_codes[:, cols].bitcast(FP8X4),
                scales=wa_scales[:, cols],
                in_=grouped[:].rearrange("p c t -> p (c t)"),
            )

        quantise_wa(0, HALF)
        picked_words = keep.tile([P, S], U32, name="picked_words")
        nc.vector.tensor_copy(picked_words[:], table_words[:].indirect(offs_sb[:]))
        x_codes = keep.tile([P, S], U32, align_bytes=64, name="x_codes")
        nc.vector.tensor_copy(
            out=x_codes[:].rearrange("p (t m) -> p m t", t=PACK),
            in_=picked_words[:].rearrange("p (m t) -> p m t", t=PACK),
        )
        quantise_wa(1, 128)

        y = [keep.tile([P, H], F32, name="y%d" % t) for t in range(PACK)]
        y_acc = {}
        for t in range(PACK):
            for f in range(2):
                cols = slice(f * HALF, (f + 1) * HALF)
                acc = psum.tile([P, HALF], F32, name="bank%d_%d" % (f, t))
                product(acc[:], (x_codes, x_scale), slice(t * P, (t + 1) * P), (wa_codes, wa_scales), cols)
                y_acc[f, t] = acc
                if f == 1 and t % 2 == 0:
                    nc.vector.tensor_scalar(y[t][:, cols], acc[:], size[:, t : t + 1], None, ALU.mult)
                else:
                    nc.scalar.activation(y[t][:, cols], acc[:], ACT.Copy, scale=size[:, t : t + 1])

        w1_grouped = keep.tile([P, N, PACK], BF16, align_bytes=64, name="w1_grouped")
        for r in range(N // P):
            engine = nc.gpsimd if r < 4 else nc.vector
            engine.tensor_tensor(
                packed_view(w1_grouped[:, r * P : (r + 1) * P, :]),
                planes_view(w1_raw[:, :, r * P : (r + 1) * P]),
                sign[:].unsqueeze(1).unsqueeze(3).to_broadcast([P, P // RUN, PACK, RUN]),
                ALU.mult,
            )

        z = []
        for f, cols in enumerate(PIECES):
            width = cols.stop - cols.start
            entries = slice(cols.start // 16, cols.stop // 16)
            first = keep.tile([P, PACK, width], F32, name="first%d" % f)
            second = keep.tile([P, PACK, width], F32, name="second%d" % f)
            larger = keep.tile([P, PACK, width], F32, name="larger%d" % f)
            for t in range(PACK):
                nc.scalar.activation(first[:, t, :], y[t][:].indirect(n1_sb[:, entries]), ACT.Copy)
            for t in range(PACK):
                if f * PACK + t < 4:
                    nc.vector.tensor_copy(second[:, t, :], y[t][:].indirect(n2_sb[:, entries]))
                else:
                    nc.scalar.activation(second[:, t, :], y[t][:].indirect(n2_sb[:, entries]), ACT.Copy)
            for t in range(PACK):
                for half in range(2):
                    lo, hi = max(cols.start, half * HALF), min(cols.stop, (half + 1) * HALF)
                    if lo < hi:
                        nc.vector.scalar_tensor_tensor(
                            larger[:, t, lo - cols.start : hi - cols.start],
                            y_acc[half, t][:, lo - half * HALF : hi - half * HALF],
                            size[:, t : t + 1],
                            first[:, t, lo - cols.start : hi - cols.start],
                            ALU.mult,
                            ALU.max,
                        )
            if f == 1:
                w1_q = quantise(w1_grouped, N, "w1")
            name = "w1_grouped" if f == 1 else "z_grouped"
            grouped = keep.tile([P, width, PACK], BF16, align_bytes=64, name=name)
            nc.vector.tensor_tensor(packed_view(grouped[:]), planes_view(larger[:]), planes_view(second[:]), ALU.min)
            z.append(quantise(grouped, width, "z%d" % f))

        tiles = range(N // P)
        h = [keep.tile([P, H], F32, name="h%d" % r) for r in tiles]
        h_acc = {}
        for f, cols in enumerate(PIECES):
            width = cols.stop - cols.start
            for r in tiles:
                h_acc[f, r] = psum.tile([P, width], F32, name="bank%d_%d" % (f, r))
                for a in range(0, width, HALF):
                    part = slice(a, min(a + HALF, width))
                    product(h_acc[f, r][:, part], w1_q, slice(r * P, (r + 1) * P), z[f], part)
                if f == 0 and r < 4:
                    nc.scalar.copy(h[r][:, cols], h_acc[f, r][:])
        old = [keep.tile([P, W], F32, name="old%d" % r) for r in tiles]
        pa = [keep.tile([P, W], F32, name="pa%d" % r) for r in tiles]
        root = [keep.tile([P, W], F32, name="root%d" % r) for r in tiles]
        ra = {}

        def fetch(r):
            if r >= 4:
                nc.vector.tensor_copy(h[r][:, PIECES[0]], h_acc[0, r][:])
            nc.vector.tensor_copy(h[r][:, PIECES[1]], h_acc[1, r][:])
            nc.scalar.activation(old[r][:], h[r][:].indirect(n3_sb[:]), ACT.Copy)

        def fetch_sizes(r):
            signed = keep.tile([P, W], F32, name="signed" if r < 2 else "part%d" % (r - 2))
            nc.vector.tensor_copy(signed[:], h[r][:].indirect(n4_sb[:]))
            nc.vector.scalar_tensor_tensor(pa[r][:], signed[:], -1.0, signed[:], ALU.mult, ALU.max)

        def invert(r):
            cut = W - 0 if r == 3 else W
            if cut > 0:
                nc.scalar.activation(root[r][:, :cut], pa[r][:, :cut], ACT.Abs_reciprocal_sqrt, bias=0.5)

        def multiply(r):
            cut = W - 0 if r == 3 else W
            part = keep.tile([P, W], F32, name="part%d" % r)
            ra[r] = keep.tile([P, W], F32, name="signed" if r == 0 else "part%d" % (r - 1))
            step = W // 2 if r < 1 else W
            if cut < W:
                nc.vector.tensor_scalar(part[:, cut:], pa[r][:, cut:], 0.5, None, ALU.add)
                nc.vector.reciprocal(root[r][:, cut:], part[:, cut:])
                nc.vector.tensor_tensor(ra[r][:, cut:], old[r][:, cut:], root[r][:, cut:], ALU.mult)
            for a in range(0, cut, step):
                b = min(a + step, cut)
                nc.vector.tensor_tensor(part[:, a:b], old[r][:, a:b], root[r][:, a:b], ALU.mult)
            for a in range(0, cut, step):
                b = min(a + step, cut)
                nc.vector.tensor_tensor(ra[r][:, a:b], part[:, a:b], root[r][:, a:b], ALU.mult)

        def put(r):
            nc.scalar.activation(h[r][:].indirect(n3_sb[:]), ra[r][:], ACT.Copy)
            nc.sync.dma_start(out=out[r * P : (r + 1) * P, :], in_=h[r][:])

        fetch(0)
        fetch(1)
        fetch_sizes(0)
        fetch(2)
        invert(0)
        fetch_sizes(1)
        invert(1)
        fetch(3)
        multiply(0)
        put(0)
        fetch_sizes(2)
        invert(2)
        multiply(1)
        put(1)
        fetch_sizes(3)
        invert(3)
        multiply(2)
        put(2)
        multiply(3)
        put(3)
